import numpy as np
import ml_dtypes


def mxq(x, axis, fmt="e4m3"):
    dtype, down = {"e4m3": (ml_dtypes.float8_e4m3fn, 7), "e5m2": (ml_dtypes.float8_e5m2, 14)}[fmt]
    v = np.moveaxis(np.asarray(x, np.float32).astype(ml_dtypes.bfloat16).astype(np.float64), axis, -1)
    blocks = v.reshape(v.shape[:-1] + (-1, 32))
    amax = np.abs(blocks).max(-1, keepdims=True)
    byte = np.maximum(np.where(amax > 0, np.frexp(amax)[1] - 1 + 127, 0) - down, 1)
    scale = np.exp2(byte - 127.0)
    codes = (blocks / scale).astype(np.float32).astype(dtype).astype(np.float64)
    return np.moveaxis((codes * scale).reshape(v.shape), -1, axis)


WIDE = False


def mx_kscale(k, group=512):
    if not WIDE:
        return np.ones(k)
    levels = np.array([10, -10, 5, -5, 0])
    if group != 512:
        return np.exp2(np.random.permutation(np.resize(levels, k // group))).repeat(group)
    if k % 512:
        return np.exp2(np.random.permutation(np.resize(levels, k // 32))).repeat(32)
    a = np.empty((k // 512, 16))
    for p in range(k // 512):
        a[p, :8] = np.random.permutation(np.resize(levels, 8))
        for g in range(8):
            far = levels[np.abs(levels - a[p, g]) >= 10]
            a[p, g + 8] = far[np.random.randint(len(far))]
    return np.exp2(a.ravel()).repeat(32)


def f64(x):
    return np.asarray(x).astype(np.float64)


def striped(idx):
    return np.tile(np.asarray(idx).reshape(-1, 16).T, (8, 1)).astype(np.uint16)


def unstriped(offs):
    return offs[:16].T.reshape(-1).astype(np.int64)


H, KV, D, NQ, N = 4, 2, 256, 512, 512
CAP = 2.0


def setup_inputs():
    n = np.random.standard_normal
    s = mx_kscale(D, 0)[:, None]
    u = mx_kscale(N)
    t = np.random.uniform(0.5, 2.0, N) * u
    v = n((KV, N, 128))
    return {
        "qT": (n((H, D, NQ)) * s * (0.70 / np.sqrt(D))).astype(np.float32),
        "kT": (n((KV, D, N)) / s).astype(np.float32),
        "t": t.reshape(N, 1).astype(np.float32),
        "v": (v / t[:, None]).astype(np.float32),
        "gn": np.tile(np.random.uniform(0.5, 2.0, 128), (128, 1)).astype(np.float32),
        "og": n((H, NQ, 128)).astype(np.float32),
    }


def reference(qT, kT, t, v, gn, og):
    a = np.repeat(mxq(f64(kT), 1, "e4m3"), H // KV, 0).transpose(0, 2, 1) @ mxq(f64(qT), 1, "e4m3")
    a = CAP * np.tanh(a / CAP)
    p = np.maximum(a, 0.0)
    w = p * f64(t)
    y = mxq(w, 1, "e4m3").transpose(0, 2, 1) @ np.repeat(mxq(f64(v), 1, "e4m3"), H // KV, 0)
    y = y / 16.0
    y = y / np.sqrt(np.mean(np.square(y), -1, keepdims=True) + 1e-5) * f64(gn)[:1]
    y = y / (1.0 + np.exp(-f64(og)))
    return y

@@ -1,0 +1,299 @@
+from contextlib import ExitStack
+
+import concourse.mybir as mybir
+
+H, KV, D, NQ, N, E = 4, 2, 256, 512, 512, 128
+FLOPS = 2 * H * N * NQ * D + 2 * H * NQ * N * E
+
+F32 = mybir.dt.float32
+BF16 = mybir.dt.bfloat16
+U32 = mybir.dt.uint32
+U8 = mybir.dt.uint8
+FP8X4 = mybir.dt.float8_e4m3fn_x4
+ACT = mybir.ActivationFunctionType
+ALU = mybir.AluOpType
+
+P = 128
+PACK = 4
+ROWS = 64
+QB = 128
+PAIRS = ((1, 2), (0, 3))
+BLOCKS = NQ // QB
+STEPS = len(PAIRS) * BLOCKS
+HALF = N // 2
+KB_SPLIT = 108
+SCALAR_CASTS = 6
+
+
+def tile_rows_a_relu_cap_onorm_gate_kernel(tc, qT, kT, t, v, gn, og, out):
+    nc = tc.nc
+    with ExitStack() as ctx:
+        keep = ctx.enter_context(tc.tile_pool(name="keep", bufs=1))
+        work = ctx.enter_context(tc.tile_pool(name="work", bufs=3))
+        psum = ctx.enter_context(tc.psum_pool(name="psum", bufs=1))
+        ctx.enter_context(tc.manual_schedule())
+
+        def kept(name, shape, dtype):
+            return keep.tile(shape, dtype, name=name, align_bytes=64)
+
+        k_raw = [kept("k_raw%d" % c, [P, PACK, HALF], F32) for c in range(2)]
+        q_widths = [QB, QB, 2 * QB, 2 * QB, 2 * QB]
+        q_raw = [kept("q_raw%d" % c, [P, PACK, w], F32) for c, w in enumerate(q_widths)]
+        q_src = [(0, 0), (1, 0), (2, 0), (2, QB), (3, 0), (3, QB), (4, 0), (4, QB)]
+        v_raw = kept("v_raw", [P, KV, PACK, E], F32)
+        og_raw = [kept("og_raw%d" % c, [P, 2, BLOCKS, E], F32) for c in range(2)]
+        t_raw = kept("t_raw", [P, PACK], F32)
+        t2 = kept("t2", [P, PACK], F32)
+        gn_sb = kept("gn_sb", [P, E], F32)
+        zeros = kept("zeros", [P, 1], F32)
+        twos = kept("twos", [P, 1], F32)
+
+        k_bf = kept("k_bf", [P, PACK, P, PACK], BF16)
+        k_codes = kept("k_codes", [P, PACK, P], U32)
+        k_scales = kept("k_scales", [P, PACK, P], U8)
+        v_bf = kept("v_bf", [P, KV, E, PACK], BF16)
+        v_codes = kept("v_codes", [P, KV, E], U32)
+        v_scales = kept("v_scales", [P, KV, E], U8)
+
+        score = [[psum.tile([P, PACK, QB], F32, name="score%d_%d" % (g, s)) for s in range(2)] for g in range(2)]
+        ybank = [psum.tile([P, 2, 2, E], F32, name="ybank%d" % s) for s in range(4)]
+
+        q_bf, q_codes, q_scales, capped, w_bf, w_codes, w_scales = {}, {}, {}, {}, {}, {}, {}
+        sums, means, factor, gate_t, gate, result = {}, {}, {}, {}, {}, {}
+
+        k_rows = kT.rearrange("h (p j) n -> (h p) j n", j=PACK)
+        qa_rows = qT[1:3].rearrange("h (p j) n -> (h p) j n", j=PACK)
+        nc.scalar.dma_start(out=t_raw[:], in_=t.rearrange("(p r) o -> p (r o)", r=PACK))
+        nc.gpsimd.memset(zeros[:], 0.0)
+        nc.scalar.activation(out=twos[:], in_=zeros[:], func=ACT.Copy, bias=2.0, scale=1.0)
+        nc.vector.tensor_scalar(out=t2[:], in0=t_raw[:], scalar1=twos[:], scalar2=0.0, op0=ALU.mult, op1=ALU.add)
+
+        nc.sync.dma_start(out=k_raw[0][:], in_=k_rows[:, :, 0:HALF])
+        nc.sync.dma_start(out=q_raw[0][:], in_=qa_rows[:, :, 0:QB])
+        nc.sync.dma_start(out=k_raw[1][:], in_=k_rows[:, :, HALF:N])
+        nc.sync.dma_start(out=q_raw[1][:], in_=qa_rows[:, :, QB : 2 * QB])
+        nc.sync.dma_start(out=q_raw[2][:], in_=qa_rows[:, :, 2 * QB : NQ])
+        nc.sync.dma_start(
+            out=v_raw[:].rearrange("p g j e -> p g (j e)"), in_=v.rearrange("g (p j) e -> p g (j e)", j=PACK)
+        )
+
+        def load_far_pair(c):
+            for g in range(2):
+                head_rows = qT[PAIRS[1][g]].rearrange("(p j) n -> p j n", j=PACK)
+                nc.sync.dma_start(
+                    out=q_raw[3 + c][ROWS * g : ROWS * (g + 1)], in_=head_rows[:, :, 2 * QB * c : 2 * QB * (c + 1)]
+                )
+
+        load_far_pair(0)
+        nc.sync.dma_start(
+            out=og_raw[0][:].rearrange("p g b e -> p (g b) e"), in_=og[1:3].rearrange("h (b p) e -> p (h b) e", p=P)
+        )
+        nc.sync.dma_start(out=gn_sb[:], in_=gn)
+        load_far_pair(1)
+        for g in range(2):
+            nc.sync.dma_start(out=og_raw[1][:, g], in_=og[PAIRS[1][g]].rearrange("(b p) e -> p b e", p=P))
+
+        def cast(on_scalar, dst, src):
+            if on_scalar:
+                nc.scalar.copy(out=dst, in_=src)
+            else:
+                nc.vector.tensor_copy(out=dst, in_=src)
+
+        def interleave(on_scalar, dst, src):
+            cast(
+                on_scalar,
+                dst.rearrange("p (c i) j -> p c j i", i=PACK),
+                src.rearrange("p j (c i) -> p c j i", i=PACK),
+            )
+
+        def quantize(codes, scales, values):
+            nc.vector.quantize_mx(out=codes.bitcast(FP8X4), scales=scales, in_=values)
+
+        def deal_keys(on_scalar, s0, s1):
+            c = s0 // ROWS
+            src = k_raw[c][:].rearrange("p j (s r) -> p s j r", r=PACK)[:, s0 - ROWS * c : s1 - ROWS * c]
+            cast(on_scalar, k_bf[:].rearrange("p r s j -> p s j r")[:, s0:s1], src)
+
+        def quantize_keys(c):
+            cols = slice(ROWS * c, ROWS * (c + 1))
+            for r in range(PACK):
+                quantize(k_codes[:, r, cols], k_scales[:, r, cols], k_bf[:, r, cols, :].rearrange("p s j -> p (s j)"))
+
+        def cast_queries(i, on_scalar):
+            c, col = q_src[i]
+            q_bf[i] = work.tile([P, QB, PACK], BF16, name="q_bf", align_bytes=64)
+            interleave(on_scalar, q_bf[i][:], q_raw[c][:, :, col : col + QB])
+
+        def quantize_queries(i):
+            q_codes[i] = work.tile([P, QB], U32, name="q_codes", align_bytes=64)
+            q_scales[i] = work.tile([P, QB], U8, name="q_scales", align_bytes=64)
+            quantize(q_codes[i][:], q_scales[i][:], q_bf[i][:].rearrange("p q j -> p (q j)"))
+
+        def scores(i):
+            for r in range(PACK):
+                for g in range(2):
+                    rows = slice(ROWS * g, ROWS * (g + 1))
+                    nc.tensor.matmul_mx(
+                        out=score[g][i % 2][:, r, :],
+                        lhsT=k_codes[rows, r, :].bitcast(FP8X4),
+                        lhsT_scale=k_scales[rows, r, :],
+                        rhs=q_codes[i][rows, :].bitcast(FP8X4),
+                        rhs_scale=q_scales[i][rows, :],
+                        start=True,
+                        stop=True,
+                    )
+
+        def cap(i, g):
+            capped[i, g] = work.tile([P, QB, PACK], F32, name="capped", bufs=6)
+            nc.scalar.activation(
+                out=capped[i, g][:], in_=score[g][i % 2][:].rearrange("p r q -> p q r"), func=ACT.Tanh, scale=0.5
+            )
+
+        def weigh(i, g):
+            if g == 0:
+                w_bf[i] = work.tile([P, 2, QB, PACK], BF16, name="w_bf", align_bytes=64)
+            nc.vector.scalar_tensor_tensor(
+                out=w_bf[i][:, g],
+                in0=capped[i, g][:],
+                scalar=0.0,
+                in1=t2[:].unsqueeze(1).to_broadcast([P, QB, PACK]),
+                op0=ALU.max,
+                op1=ALU.mult,
+            )
+
+        def quantize_weights(i):
+            w_codes[i] = work.tile([P, 2, QB], U32, name="w_codes", align_bytes=64, bufs=4)
+            w_scales[i] = work.tile([P, 2, QB], U8, name="w_scales", align_bytes=64, bufs=4)
+            quantize(
+                w_codes[i][:].rearrange("p g q -> p (g q)"),
+                w_scales[i][:].rearrange("p g q -> p (g q)"),
+                w_bf[i][:].rearrange("p g q j -> p (g q j)"),
+            )
+
+        def mix(i):
+            for g in range(2):
+                nc.tensor.matmul_mx(
+                    out=ybank[i // 2][:, i % 2, g, :],
+                    lhsT=w_codes[i][:, g, :].bitcast(FP8X4),
+                    lhsT_scale=w_scales[i][:, g, :],
+                    rhs=v_codes[:, g, :].bitcast(FP8X4),
+                    rhs_scale=v_scales[:, g, :],
+                    start=True,
+                    stop=True,
+                )
+
+        def sum_squares(i):
+            if i % 2 == 0:
+                sums[i // 2] = work.tile([P, 2, 2], F32, name="sums", bufs=4)
+            for g in range(2):
+                squares = work.tile([P, E], F32, name="squares")
+                nc.scalar.activation(
+                    out=squares[:],
+                    in_=ybank[i // 2][:, i % 2, g, :],
+                    func=ACT.Square,
+                    accum_out=sums[i // 2][:, i % 2, g : g + 1],
+                )
+
+        def root(n):
+            means[n] = work.tile([P, 2, 2], F32, name="means", bufs=4)
+            nc.scalar.activation(out=means[n][:], in_=sums[n][:], func=ACT.Sqrt, scale=1.0 / 32.0, bias=1024e-5)
+
+        def norm_factor(n):
+            factor[n] = work.tile([P, 2, 2], F32, name="factor", bufs=4)
+            nc.vector.reciprocal(out=factor[n][:], in_=means[n][:])
+
+        def gate_tanh(u):
+            gate_t[u] = work.tile([P, BLOCKS, E], F32, name="gate_t", bufs=4)
+            nc.scalar.activation(out=gate_t[u][:], in_=og_raw[u // 2][:, u % 2], func=ACT.Tanh, scale=0.5)
+
+        def gate_gain(u):
+            gate[u] = work.tile([P, BLOCKS, E], F32, name="gate", bufs=4)
+            nc.vector.scalar_tensor_tensor(
+                out=gate[u][:],
+                in0=gate_t[u][:],
+                scalar=1.0,
+                in1=gn_sb[:].unsqueeze(1).to_broadcast([P, BLOCKS, E]),
+                op0=ALU.add,
+                op1=ALU.mult,
+            )
+
+        def finish(i):
+            result[i] = work.tile([P, 2, E], F32, name="result", bufs=8)
+            for g in range(2):
+                nc.vector.scalar_tensor_tensor(
+                    out=result[i][:, g, :],
+                    in0=ybank[i // 2][:, i % 2, g, :],
+                    scalar=factor[i // 2][:, i % 2, g : g + 1],
+                    in1=gate[2 * (i // BLOCKS) + g][:, i % BLOCKS, :],
+                    op0=ALU.mult,
+                    op1=ALU.mult,
+                )
+            first, second = PAIRS[i // BLOCKS]
+            q0 = QB * (i % BLOCKS)
+            heads = out[first : second + 1 : second - first, q0 : q0 + QB, :]
+            nc.sync.dma_start(out=heads.rearrange("h q e -> q h e"), in_=result[i][:])
+
+        deal_keys(False, 0, ROWS)
+        cast_queries(0, True)
+        quantize_keys(0)
+        quantize_queries(0)
+        deal_keys(True, KB_SPLIT, P)
+        deal_keys(False, ROWS, KB_SPLIT)
+        quantize_keys(1)
+        scores(0)
+        cast_queries(1, True)
+        quantize_queries(1)
+        scores(1)
+
+        for i in range(STEPS):
+            ahead = i + 2
+            if i == STEPS - 1:
+                gate_tanh(i - 4)
+            cap(i, 0)
+            cap(i, 1)
+            if ahead < SCALAR_CASTS:
+                cast_queries(ahead, True)
+            if 4 <= i < STEPS - 1:
+                gate_tanh(i - 4)
+            if i in (5, 6):
+                sum_squares(i - 5)
+            weigh(i, 0)
+            if SCALAR_CASTS <= ahead < STEPS:
+                cast_queries(ahead, False)
+            if i == 1:
+                for g in range(KV):
+                    interleave(False, v_bf[:, g], v_raw[:, g])
+            weigh(i, 1)
+            if ahead < STEPS:
+                quantize_queries(ahead)
+                scores(ahead)
+            if i == 1:
+                quantize(
+                    v_codes[:].rearrange("p g e -> p (g e)"),
+                    v_scales[:].rearrange("p g e -> p (g e)"),
+                    v_bf[:].rearrange("p g e j -> p (g e j)"),
+                )
+            if i >= STEPS - 2:
+                gate_gain(i - (STEPS - 2))
+            quantize_weights(i)
+            if i >= 1:
+                mix(i - 1)
+        mix(STEPS - 1)
+
+        root(0)
+        gate_gain(2)
+        norm_factor(0)
+        for n in range(1, 4):
+            if n == 1:
+                sum_squares(2)
+            sum_squares(2 * n + 1)
+            if n < 3:
+                sum_squares(2 * n + 2)
+            root(n)
+            finish(2 * n - 2)
+            finish(2 * n - 1)
+            if n == 1:
+                gate_gain(3)
+            norm_factor(n)
+        finish(6)
+        finish(7)

@@ -17,91 +17,101 @@ P = 128
 PACK = 4
 ROWS = 64
 QB = 128
+CHUNK = 2 * QB
 PAIRS = ((1, 2), (0, 3))
 BLOCKS = NQ // QB
 STEPS = len(PAIRS) * BLOCKS
-HALF = N // 2
-KB_SPLIT = 108
-SCALAR_CASTS = 6
+KEY_SPLIT = 84
 
 
 def tile_rows_a_relu_cap_onorm_gate_kernel(tc, qT, kT, t, v, gn, og, out):
     nc = tc.nc
     with ExitStack() as ctx:
-        keep = ctx.enter_context(tc.tile_pool(name="keep", bufs=1))
-        work = ctx.enter_context(tc.tile_pool(name="work", bufs=3))
+        sbuf = ctx.enter_context(tc.tile_pool(name="sbuf", bufs=1))
         psum = ctx.enter_context(tc.psum_pool(name="psum", bufs=1))
         ctx.enter_context(tc.manual_schedule())
 
-        def kept(name, shape, dtype):
-            return keep.tile(shape, dtype, name=name, align_bytes=64)
+        def one(name, shape, dtype):
+            return sbuf.tile(shape, dtype, name=name, align_bytes=64)
 
-        k_raw = [kept("k_raw%d" % c, [P, PACK, HALF], F32) for c in range(2)]
-        q_widths = [QB, QB, 2 * QB, 2 * QB, 2 * QB]
-        q_raw = [kept("q_raw%d" % c, [P, PACK, w], F32) for c, w in enumerate(q_widths)]
-        q_src = [(0, 0), (1, 0), (2, 0), (2, QB), (3, 0), (3, QB), (4, 0), (4, QB)]
-        v_raw = kept("v_raw", [P, KV, PACK, E], F32)
-        og_raw = [kept("og_raw%d" % c, [P, 2, BLOCKS, E], F32) for c in range(2)]
-        t_raw = kept("t_raw", [P, PACK], F32)
-        t2 = kept("t2", [P, PACK], F32)
-        gn_sb = kept("gn_sb", [P, E], F32)
-        zeros = kept("zeros", [P, 1], F32)
-        twos = kept("twos", [P, 1], F32)
+        def many(name, count, shape, dtype):
+            return [one("%s%d" % (name, n), shape, dtype) for n in range(count)]
 
-        k_bf = kept("k_bf", [P, PACK, P, PACK], BF16)
-        k_codes = kept("k_codes", [P, PACK, P], U32)
-        k_scales = kept("k_scales", [P, PACK, P], U8)
-        v_bf = kept("v_bf", [P, KV, E, PACK], BF16)
-        v_codes = kept("v_codes", [P, KV, E], U32)
-        v_scales = kept("v_scales", [P, KV, E], U8)
+        chunks = STEPS // 2
+        k_raw = one("k_raw", [P, PACK, N], F32)
+        q_raw = many("q_raw", chunks, [P, PACK, CHUNK], F32)
+        v_raw = one("v_raw", [P, KV, PACK, E], F32)
+        og_raw = many("og_raw", H, [P, BLOCKS, E], F32)
+        t_raw = one("t_raw", [P, PACK], F32)
+        gn_sb = one("gn_sb", [P, E], F32)
+        zeros = one("zeros", [P, 1], F32)
+        twos = one("twos", [P, 1], F32)
+        t2 = one("t2", [P, PACK], F32)
 
-        score = [[psum.tile([P, PACK, QB], F32, name="score%d_%d" % (g, s)) for s in range(2)] for g in range(2)]
-        ybank = [psum.tile([P, 2, 2, E], F32, name="ybank%d" % s) for s in range(4)]
+        k_bf = one("k_bf", [P, PACK, P, PACK], BF16)
+        k_codes = one("k_codes", [P, PACK, P], U32)
+        k_scales = one("k_scales", [P, PACK, P], U8)
+        q_bf = many("q_bf", chunks, [P, CHUNK, PACK], BF16)
+        q_codes = many("q_codes", chunks, [P, CHUNK], U32)
+        q_scales = many("q_scales", chunks, [P, CHUNK], U8)
+        v_bf = one("v_bf", [P, KV, E, PACK], BF16)
+        v_codes = one("v_codes", [P, KV, E], U32)
+        v_scales = one("v_scales", [P, KV, E], U8)
 
-        q_bf, q_codes, q_scales, capped, w_bf, w_codes, w_scales = {}, {}, {}, {}, {}, {}, {}
-        sums, means, factor, gate_t, gate, result = {}, {}, {}, {}, {}, {}
+        capped = many("capped", STEPS, [P, 2, QB, PACK], F32)
+        w_bf = many("w_bf", STEPS, [P, 2, QB, PACK], BF16)
+        w_codes = many("w_codes", STEPS, [P, 2, QB], U32)
+        w_scales = many("w_scales", STEPS, [P, 2, QB], U8)
+        squares = many("squares", STEPS, [P, 2, E], F32)
+        sums = many("sums", chunks, [P, 2, 2], F32)
+        factor = many("factor", chunks, [P, 2, 2], F32)
+        gate_tanh = many("gate_tanh", H, [P, BLOCKS, E], F32)
+        gate = many("gate", H, [P, BLOCKS, E], F32)
+        result = many("result", STEPS, [P, 2, E], F32)
 
-        k_rows = kT.rearrange("h (p j) n -> (h p) j n", j=PACK)
-        qa_rows = qT[1:3].rearrange("h (p j) n -> (h p) j n", j=PACK)
-        nc.scalar.dma_start(out=t_raw[:], in_=t.rearrange("(p r) o -> p (r o)", r=PACK))
+        score = [[psum.tile([P, PACK, QB], F32, name="score%d_%d" % (g, n)) for n in range(2)] for g in range(2)]
+        ybank = [psum.tile([P, 2, 2, E], F32, name="ybank%d" % n) for n in range(chunks)]
+
         nc.gpsimd.memset(zeros[:], 0.0)
         nc.scalar.activation(out=twos[:], in_=zeros[:], func=ACT.Copy, bias=2.0, scale=1.0)
-        nc.vector.tensor_scalar(out=t2[:], in0=t_raw[:], scalar1=twos[:], scalar2=0.0, op0=ALU.mult, op1=ALU.add)
 
-        nc.sync.dma_start(out=k_raw[0][:], in_=k_rows[:, :, 0:HALF])
-        nc.sync.dma_start(out=q_raw[0][:], in_=qa_rows[:, :, 0:QB])
-        nc.sync.dma_start(out=k_raw[1][:], in_=k_rows[:, :, HALF:N])
-        nc.sync.dma_start(out=q_raw[1][:], in_=qa_rows[:, :, QB : 2 * QB])
-        nc.sync.dma_start(out=q_raw[2][:], in_=qa_rows[:, :, 2 * QB : NQ])
+        def load_queries(c):
+            pair, cols = PAIRS[c // 2], slice(CHUNK * (c % 2), CHUNK * (c % 2 + 1))
+            if pair[1] == pair[0] + 1:
+                rows = qT[pair[0] : pair[1] + 1].rearrange("h (p j) n -> (h p) j n", j=PACK)
+                nc.sync.dma_start(out=q_raw[c][:], in_=rows[:, :, cols])
+            else:
+                for g in range(2):
+                    rows = qT[pair[g]].rearrange("(p j) n -> p j n", j=PACK)
+                    nc.sync.dma_start(out=q_raw[c][ROWS * g : ROWS * (g + 1)], in_=rows[:, :, cols])
+
+        def load_gate(u):
+            nc.sync.dma_start(out=og_raw[u][:], in_=og[PAIRS[u // 2][u % 2]].rearrange("(b p) e -> p b e", p=P))
+
+        nc.sync.dma_start(out=k_raw[:], in_=kT.rearrange("h (p j) n -> (h p) j n", j=PACK))
+        load_queries(0)
+        nc.sync.dma_start(out=t_raw[:], in_=t.rearrange("(p r) o -> p (r o)", r=PACK))
+        load_queries(1)
         nc.sync.dma_start(
             out=v_raw[:].rearrange("p g j e -> p g (j e)"), in_=v.rearrange("g (p j) e -> p g (j e)", j=PACK)
         )
-
-        def load_far_pair(c):
-            for g in range(2):
-                head_rows = qT[PAIRS[1][g]].rearrange("(p j) n -> p j n", j=PACK)
-                nc.sync.dma_start(
-                    out=q_raw[3 + c][ROWS * g : ROWS * (g + 1)], in_=head_rows[:, :, 2 * QB * c : 2 * QB * (c + 1)]
-                )
-
-        load_far_pair(0)
-        nc.sync.dma_start(
-            out=og_raw[0][:].rearrange("p g b e -> p (g b) e"), in_=og[1:3].rearrange("h (b p) e -> p (h b) e", p=P)
-        )
+        load_queries(2)
+        load_queries(3)
+        load_gate(0)
+        load_gate(1)
         nc.sync.dma_start(out=gn_sb[:], in_=gn)
-        load_far_pair(1)
-        for g in range(2):
-            nc.sync.dma_start(out=og_raw[1][:, g], in_=og[PAIRS[1][g]].rearrange("(b p) e -> p b e", p=P))
+        load_gate(2)
+        load_gate(3)
 
-        def cast(on_scalar, dst, src):
-            if on_scalar:
+        def cast(engine, dst, src):
+            if engine == "scalar":
                 nc.scalar.copy(out=dst, in_=src)
             else:
                 nc.vector.tensor_copy(out=dst, in_=src)
 
-        def interleave(on_scalar, dst, src):
+        def interleave(engine, dst, src):
             cast(
-                on_scalar,
+                engine,
                 dst.rearrange("p (c i) j -> p c j i", i=PACK),
                 src.rearrange("p j (c i) -> p c j i", i=PACK),
             )
@@ -109,27 +119,39 @@ def tile_rows_a_relu_cap_onorm_gate_kernel(tc, qT, kT, t, v, gn, og, out):
         def quantize(codes, scales, values):
             nc.vector.quantize_mx(out=codes.bitcast(FP8X4), scales=scales, in_=values)
 
-        def deal_keys(on_scalar, s0, s1):
-            c = s0 // ROWS
-            src = k_raw[c][:].rearrange("p j (s r) -> p s j r", r=PACK)[:, s0 - ROWS * c : s1 - ROWS * c]
-            cast(on_scalar, k_bf[:].rearrange("p r s j -> p s j r")[:, s0:s1], src)
+        def deal_keys(engine, s0, s1):
+            src = k_raw[:].rearrange("p j (s r) -> p s j r", r=PACK)
+            cast(engine, k_bf[:].rearrange("p r s j -> p s j r")[:, s0:s1], src[:, s0:s1])
 
-        def quantize_keys(c):
-            cols = slice(ROWS * c, ROWS * (c + 1))
+        def quantize_keys(half):
+            cols = slice(P // 2 * half, P // 2 * (half + 1))
             for r in range(PACK):
                 quantize(k_codes[:, r, cols], k_scales[:, r, cols], k_bf[:, r, cols, :].rearrange("p s j -> p (s j)"))
 
-        def cast_queries(i, on_scalar):
-            c, col = q_src[i]
-            q_bf[i] = work.tile([P, QB, PACK], BF16, name="q_bf", align_bytes=64)
-            interleave(on_scalar, q_bf[i][:], q_raw[c][:, :, col : col + QB])
+        def query_cols(i, steps):
+            return slice(QB * (i % 2), QB * (i % 2 + steps))
 
-        def quantize_queries(i):
-            q_codes[i] = work.tile([P, QB], U32, name="q_codes", align_bytes=64)
-            q_scales[i] = work.tile([P, QB], U8, name="q_scales", align_bytes=64)
-            quantize(q_codes[i][:], q_scales[i][:], q_bf[i][:].rearrange("p q j -> p (q j)"))
+        def cast_queries(engine, i, steps=1):
+            cols = query_cols(i, steps)
+            interleave(engine, q_bf[i // 2][:, cols, :], q_raw[i // 2][:, :, cols])
+
+        def quantize_queries(i, steps=1):
+            cols = query_cols(i, steps)
+            values = q_bf[i // 2][:, cols, :].rearrange("p q j -> p (q j)")
+            quantize(q_codes[i // 2][:, cols], q_scales[i // 2][:, cols], values)
+
+        def cast_values(engine, g):
+            interleave(engine, v_bf[:, g], v_raw[:, g])
+
+        def quantize_values():
+            quantize(
+                v_codes[:].rearrange("p g e -> p (g e)"),
+                v_scales[:].rearrange("p g e -> p (g e)"),
+                v_bf[:].rearrange("p g e j -> p (g e j)"),
+            )
 
         def scores(i):
+            cols = query_cols(i, 1)
             for r in range(PACK):
                 for g in range(2):
                     rows = slice(ROWS * g, ROWS * (g + 1))
@@ -137,37 +159,33 @@ def tile_rows_a_relu_cap_onorm_gate_kernel(tc, qT, kT, t, v, gn, og, out):
                         out=score[g][i % 2][:, r, :],
                         lhsT=k_codes[rows, r, :].bitcast(FP8X4),
                         lhsT_scale=k_scales[rows, r, :],
-                        rhs=q_codes[i][rows, :].bitcast(FP8X4),
-                        rhs_scale=q_scales[i][rows, :],
+                        rhs=q_codes[i // 2][rows, cols].bitcast(FP8X4),
+                        rhs_scale=q_scales[i // 2][rows, cols],
                         start=True,
                         stop=True,
                     )
 
-        def cap(i, g):
-            capped[i, g] = work.tile([P, QB, PACK], F32, name="capped", bufs=6)
-            nc.scalar.activation(
-                out=capped[i, g][:], in_=score[g][i % 2][:].rearrange("p r q -> p q r"), func=ACT.Tanh, scale=0.5
-            )
+        def cap(i):
+            for g in range(2):
+                nc.scalar.activation(
+                    out=capped[i][:, g], in_=score[g][i % 2][:].rearrange("p r q -> p q r"), func=ACT.Tanh, scale=0.5
+                )
 
-        def weigh(i, g):
-            if g == 0:
-                w_bf[i] = work.tile([P, 2, QB, PACK], BF16, name="w_bf", align_bytes=64)
+        def weigh(i, g0=0, g1=2):
             nc.vector.scalar_tensor_tensor(
-                out=w_bf[i][:, g],
-                in0=capped[i, g][:],
+                out=w_bf[i][:, g0:g1].rearrange("p g q r -> p (g q) r"),
+                in0=capped[i][:, g0:g1].rearrange("p g q r -> p (g q) r"),
                 scalar=0.0,
-                in1=t2[:].unsqueeze(1).to_broadcast([P, QB, PACK]),
+                in1=t2[:].unsqueeze(1).to_broadcast([P, (g1 - g0) * QB, PACK]),
                 op0=ALU.max,
                 op1=ALU.mult,
             )
 
         def quantize_weights(i):
-            w_codes[i] = work.tile([P, 2, QB], U32, name="w_codes", align_bytes=64, bufs=4)
-            w_scales[i] = work.tile([P, 2, QB], U8, name="w_scales", align_bytes=64, bufs=4)
             quantize(
                 w_codes[i][:].rearrange("p g q -> p (g q)"),
                 w_scales[i][:].rearrange("p g q -> p (g q)"),
-                w_bf[i][:].rearrange("p g q j -> p (g q j)"),
+                w_bf[i][:].rearrange("p g q r -> p (g q r)"),
             )
 
         def mix(i):
@@ -182,43 +200,35 @@ def tile_rows_a_relu_cap_onorm_gate_kernel(tc, qT, kT, t, v, gn, og, out):
                     stop=True,
                 )
 
-        def sum_squares(i):
-            if i % 2 == 0:
-                sums[i // 2] = work.tile([P, 2, 2], F32, name="sums", bufs=4)
-            for g in range(2):
-                squares = work.tile([P, E], F32, name="squares")
+        def sum_squares(i, heads=(0, 1)):
+            for g in heads:
                 nc.scalar.activation(
-                    out=squares[:],
+                    out=squares[i][:, g, :],
                     in_=ybank[i // 2][:, i % 2, g, :],
                     func=ACT.Square,
                     accum_out=sums[i // 2][:, i % 2, g : g + 1],
                 )
 
-        def root(n):
-            means[n] = work.tile([P, 2, 2], F32, name="means", bufs=4)
-            nc.scalar.activation(out=means[n][:], in_=sums[n][:], func=ACT.Sqrt, scale=1.0 / 32.0, bias=1024e-5)
+        def norm_factor(c):
+            nc.scalar.activation(
+                out=factor[c][:], in_=sums[c][:], func=ACT.Abs_reciprocal_sqrt, scale=1.0 / 32.0, bias=1024e-5
+            )
 
-        def norm_factor(n):
-            factor[n] = work.tile([P, 2, 2], F32, name="factor", bufs=4)
-            nc.vector.reciprocal(out=factor[n][:], in_=means[n][:])
+        def gate_half_tanh(u):
+            nc.scalar.activation(out=gate_tanh[u][:], in_=og_raw[u][:], func=ACT.Tanh, scale=0.5)
 
-        def gate_tanh(u):
-            gate_t[u] = work.tile([P, BLOCKS, E], F32, name="gate_t", bufs=4)
-            nc.scalar.activation(out=gate_t[u][:], in_=og_raw[u // 2][:, u % 2], func=ACT.Tanh, scale=0.5)
-
-        def gate_gain(u):
-            gate[u] = work.tile([P, BLOCKS, E], F32, name="gate", bufs=4)
+        def gate_gain(u, b0=0, b1=BLOCKS):
             nc.vector.scalar_tensor_tensor(
-                out=gate[u][:],
-                in0=gate_t[u][:],
+                out=gate[u][:, b0:b1],
+                in0=gate_tanh[u][:, b0:b1],
                 scalar=1.0,
-                in1=gn_sb[:].unsqueeze(1).to_broadcast([P, BLOCKS, E]),
+                in1=gn_sb[:].unsqueeze(1).to_broadcast([P, b1 - b0, E]),
                 op0=ALU.add,
                 op1=ALU.mult,
             )
 
         def finish(i):
-            result[i] = work.tile([P, 2, E], F32, name="result", bufs=8)
+            pair, rows = PAIRS[i // BLOCKS], slice(QB * (i % BLOCKS), QB * (i % BLOCKS + 1))
             for g in range(2):
                 nc.vector.scalar_tensor_tensor(
                     out=result[i][:, g, :],
@@ -228,72 +238,96 @@ def tile_rows_a_relu_cap_onorm_gate_kernel(tc, qT, kT, t, v, gn, og, out):
                     op0=ALU.mult,
                     op1=ALU.mult,
                 )
-            first, second = PAIRS[i // BLOCKS]
-            q0 = QB * (i % BLOCKS)
-            heads = out[first : second + 1 : second - first, q0 : q0 + QB, :]
-            nc.sync.dma_start(out=heads.rearrange("h q e -> q h e"), in_=result[i][:])
+                if i == STEPS - 1:
+                    nc.sync.dma_start(out=out[pair[g], rows, :], in_=result[i][:, g, :])
+            if i < STEPS - 1:
+                heads = out[pair[0] : pair[1] + 1 : pair[1] - pair[0], rows, :]
+                nc.sync.dma_start(out=heads.rearrange("h q e -> q h e"), in_=result[i][:])
 
-        deal_keys(False, 0, ROWS)
-        cast_queries(0, True)
+        deal_keys("scalar", KEY_SPLIT, P)
+        deal_keys("vector", 0, P // 2)
+        deal_keys("vector", P // 2, KEY_SPLIT)
         quantize_keys(0)
-        quantize_queries(0)
-        deal_keys(True, KB_SPLIT, P)
-        deal_keys(False, ROWS, KB_SPLIT)
+        cast_queries("scalar", 1)
+        cast_queries("vector", 0)
         quantize_keys(1)
-        scores(0)
-        cast_queries(1, True)
-        quantize_queries(1)
-        scores(1)
+        for i in range(2):
+            quantize_queries(i)
+            scores(i)
+        cast_queries("vector", 2, steps=2)
+        nc.vector.tensor_scalar(out=t2[:], in0=t_raw[:], scalar1=twos[:], scalar2=0.0, op0=ALU.mult, op1=ALU.add)
+        quantize_queries(2, steps=2)
+        for i in range(2):
+            cap(i)
+            scores(i + 2)
+        cast_values("vector", 1)
+        cast_values("scalar", 0)
+        for i in range(2):
+            weigh(i, 0, 1)
+            weigh(i, 1, 2)
+        cap(2)
+        quantize_values()
+        cast_queries("vector", 4)
+        quantize_weights(0)
+        mix(0)
+        quantize_queries(4)
+        scores(4)
+        cast_queries("scalar", 5)
+        cap(3)
+        weigh(2)
+        quantize_queries(5)
+        scores(5)
+        quantize_weights(1)
+        sum_squares(0)
+        mix(1)
+        cap(4)
+        cap(5)
+        weigh(3, 0, 1)
+        weigh(3, 1, 2)
+        cast_queries("vector", 6, steps=2)
+        quantize_weights(2)
+        quantize_queries(6, steps=2)
+        scores(6)
+        scores(7)
+        mix(2)
+        sum_squares(1)
+        gate_half_tanh(0)
+        gate_half_tanh(1)
+        for i in (6, 7):
+            cap(i)
+            gate_half_tanh(i - 4)
+        for i in (4, 5):
+            weigh(i)
+            quantize_weights(i - 1)
+            mix(i - 1)
+        gate_gain(0)
+        quantize_weights(5)
+        mix(5)
+        weigh(6)
+        gate_gain(1)
+        quantize_weights(6)
+        mix(6)
+        weigh(7)
 
-        for i in range(STEPS):
-            ahead = i + 2
-            if i == STEPS - 1:
-                gate_tanh(i - 4)
-            cap(i, 0)
-            cap(i, 1)
-            if ahead < SCALAR_CASTS:
-                cast_queries(ahead, True)
-            if 4 <= i < STEPS - 1:
-                gate_tanh(i - 4)
-            if i in (5, 6):
-                sum_squares(i - 5)
-            weigh(i, 0)
-            if SCALAR_CASTS <= ahead < STEPS:
-                cast_queries(ahead, False)
-            if i == 1:
-                for g in range(KV):
-                    interleave(False, v_bf[:, g], v_raw[:, g])
-            weigh(i, 1)
-            if ahead < STEPS:
-                quantize_queries(ahead)
-                scores(ahead)
-            if i == 1:
-                quantize(
-                    v_codes[:].rearrange("p g e -> p (g e)"),
-                    v_scales[:].rearrange("p g e -> p (g e)"),
-                    v_bf[:].rearrange("p g e j -> p (g e j)"),
-                )
-            if i >= STEPS - 2:
-                gate_gain(i - (STEPS - 2))
-            quantize_weights(i)
-            if i >= 1:
-                mix(i - 1)
-        mix(STEPS - 1)
-
-        root(0)
-        gate_gain(2)
         norm_factor(0)
-        for n in range(1, 4):
-            if n == 1:
-                sum_squares(2)
-            sum_squares(2 * n + 1)
-            if n < 3:
-                sum_squares(2 * n + 2)
-            root(n)
-            finish(2 * n - 2)
-            finish(2 * n - 1)
-            if n == 1:
-                gate_gain(3)
-            norm_factor(n)
-        finish(6)
-        finish(7)
+        gate_gain(2, 0, 2)
+        finish(0)
+        quantize_weights(7)
+        mix(7)
+        finish(1)
+        for c in (1, 2):
+            sum_squares(2 * c, heads=(0, 1) if c == 1 else (1,))
+            sum_squares(2 * c + 1)
+            sum_squares(2 * c + 2, heads=(0,))
+            norm_factor(c)
+        sum_squares(6, heads=(1,))
+        sum_squares(7)
+        norm_factor(3)
+        gate_gain(3, 0, 2)
+        finish(2)
+        finish(3)
+        gate_gain(2, 2, 4)
+        finish(4)
+        gate_gain(3, 2, 4)
+        for i in (5, 6, 7):
+            finish(i)

@@ -238,11 +238,8 @@ def tile_rows_a_relu_cap_onorm_gate_kernel(tc, qT, kT, t, v, gn, og, out):
                     op0=ALU.mult,
                     op1=ALU.mult,
                 )
-                if i == STEPS - 1:
-                    nc.sync.dma_start(out=out[pair[g], rows, :], in_=result[i][:, g, :])
-            if i < STEPS - 1:
-                heads = out[pair[0] : pair[1] + 1 : pair[1] - pair[0], rows, :]
-                nc.sync.dma_start(out=heads.rearrange("h q e -> q h e"), in_=result[i][:])
+            heads = out[pair[0] : pair[1] + 1 : pair[1] - pair[0], rows, :]
+            nc.sync.dma_start(out=heads.rearrange("h q e -> q h e"), in_=result[i][:])
 
         deal_keys("scalar", KEY_SPLIT, P)
         deal_keys("vector", 0, P // 2)
@@ -254,14 +251,15 @@ def tile_rows_a_relu_cap_onorm_gate_kernel(tc, qT, kT, t, v, gn, og, out):
         for i in range(2):
             quantize_queries(i)
             scores(i)
-        cast_queries("vector", 2, steps=2)
+        cast_queries("scalar", 2)
+        cast_queries("vector", 3)
         nc.vector.tensor_scalar(out=t2[:], in0=t_raw[:], scalar1=twos[:], scalar2=0.0, op0=ALU.mult, op1=ALU.add)
         quantize_queries(2, steps=2)
         for i in range(2):
             cap(i)
             scores(i + 2)
         cast_values("vector", 1)
-        cast_values("scalar", 0)
+        cast_values("vector", 0)
         for i in range(2):
             weigh(i, 0, 1)
             weigh(i, 1, 2)
@@ -311,9 +309,9 @@ def tile_rows_a_relu_cap_onorm_gate_kernel(tc, qT, kT, t, v, gn, og, out):
 
         norm_factor(0)
         gate_gain(2, 0, 2)
-        finish(0)
         quantize_weights(7)
         mix(7)
+        finish(0)
         finish(1)
         for c in (1, 2):
             sum_squares(2 * c, heads=(0, 1) if c == 1 else (1,))

from contextlib import ExitStack

import concourse.mybir as mybir

H, KV, D, NQ, N, E = 4, 2, 256, 512, 512, 128
FLOPS = 2 * H * N * NQ * D + 2 * H * NQ * N * E

F32 = mybir.dt.float32
BF16 = mybir.dt.bfloat16
U32 = mybir.dt.uint32
U8 = mybir.dt.uint8
FP8X4 = mybir.dt.float8_e4m3fn_x4
ACT = mybir.ActivationFunctionType
ALU = mybir.AluOpType

P = 128
PACK = 4
ROWS = 64
QB = 128
CHUNK = 2 * QB
PAIRS = ((1, 2), (0, 3))
BLOCKS = NQ // QB
STEPS = len(PAIRS) * BLOCKS
KEY_SPLIT = 84


def tile_rows_a_relu_cap_onorm_gate_kernel(tc, qT, kT, t, v, gn, og, out):
    nc = tc.nc
    with ExitStack() as ctx:
        sbuf = ctx.enter_context(tc.tile_pool(name="sbuf", bufs=1))
        psum = ctx.enter_context(tc.psum_pool(name="psum", bufs=1))
        ctx.enter_context(tc.manual_schedule())

        def one(name, shape, dtype):
            return sbuf.tile(shape, dtype, name=name, align_bytes=64)

        def many(name, count, shape, dtype):
            return [one("%s%d" % (name, n), shape, dtype) for n in range(count)]

        chunks = STEPS // 2
        k_raw = one("k_raw", [P, PACK, N], F32)
        q_raw = many("q_raw", chunks, [P, PACK, CHUNK], F32)
        v_raw = one("v_raw", [P, KV, PACK, E], F32)
        og_raw = many("og_raw", H, [P, BLOCKS, E], F32)
        t_raw = one("t_raw", [P, PACK], F32)
        gn_sb = one("gn_sb", [P, E], F32)
        zeros = one("zeros", [P, 1], F32)
        twos = one("twos", [P, 1], F32)
        t2 = one("t2", [P, PACK], F32)

        k_bf = one("k_bf", [P, PACK, P, PACK], BF16)
        k_codes = one("k_codes", [P, PACK, P], U32)
        k_scales = one("k_scales", [P, PACK, P], U8)
        q_bf = many("q_bf", chunks, [P, CHUNK, PACK], BF16)
        q_codes = many("q_codes", chunks, [P, CHUNK], U32)
        q_scales = many("q_scales", chunks, [P, CHUNK], U8)
        v_bf = one("v_bf", [P, KV, E, PACK], BF16)
        v_codes = one("v_codes", [P, KV, E], U32)
        v_scales = one("v_scales", [P, KV, E], U8)

        capped = many("capped", STEPS, [P, 2, QB, PACK], F32)
        w_bf = many("w_bf", STEPS, [P, 2, QB, PACK], BF16)
        w_codes = many("w_codes", STEPS, [P, 2, QB], U32)
        w_scales = many("w_scales", STEPS, [P, 2, QB], U8)
        squares = many("squares", STEPS, [P, 2, E], F32)
        sums = many("sums", chunks, [P, 2, 2], F32)
        factor = many("factor", chunks, [P, 2, 2], F32)
        gate_tanh = many("gate_tanh", H, [P, BLOCKS, E], F32)
        gate = many("gate", H, [P, BLOCKS, E], F32)
        result = many("result", STEPS, [P, 2, E], F32)

        score = [[psum.tile([P, PACK, QB], F32, name="score%d_%d" % (g, n)) for n in range(2)] for g in range(2)]
        ybank = [psum.tile([P, 2, 2, E], F32, name="ybank%d" % n) for n in range(chunks)]

        nc.gpsimd.memset(zeros[:], 0.0)
        nc.scalar.activation(out=twos[:], in_=zeros[:], func=ACT.Copy, bias=2.0, scale=1.0)

        def load_queries(c):
            pair, cols = PAIRS[c // 2], slice(CHUNK * (c % 2), CHUNK * (c % 2 + 1))
            if pair[1] == pair[0] + 1:
                rows = qT[pair[0] : pair[1] + 1].rearrange("h (p j) n -> (h p) j n", j=PACK)
                nc.sync.dma_start(out=q_raw[c][:], in_=rows[:, :, cols])
            else:
                for g in range(2):
                    rows = qT[pair[g]].rearrange("(p j) n -> p j n", j=PACK)
                    nc.sync.dma_start(out=q_raw[c][ROWS * g : ROWS * (g + 1)], in_=rows[:, :, cols])

        def load_gate(u):
            nc.sync.dma_start(out=og_raw[u][:], in_=og[PAIRS[u // 2][u % 2]].rearrange("(b p) e -> p b e", p=P))

        nc.sync.dma_start(out=k_raw[:], in_=kT.rearrange("h (p j) n -> (h p) j n", j=PACK))
        load_queries(0)
        nc.sync.dma_start(out=t_raw[:], in_=t.rearrange("(p r) o -> p (r o)", r=PACK))
        load_queries(1)
        nc.sync.dma_start(
            out=v_raw[:].rearrange("p g j e -> p g (j e)"), in_=v.rearrange("g (p j) e -> p g (j e)", j=PACK)
        )
        load_queries(2)
        load_queries(3)
        load_gate(0)
        load_gate(1)
        nc.sync.dma_start(out=gn_sb[:], in_=gn)
        load_gate(2)
        load_gate(3)

        def cast(engine, dst, src):
            if engine == "scalar":
                nc.scalar.copy(out=dst, in_=src)
            else:
                nc.vector.tensor_copy(out=dst, in_=src)

        def interleave(engine, dst, src):
            cast(
                engine,
                dst.rearrange("p (c i) j -> p c j i", i=PACK),
                src.rearrange("p j (c i) -> p c j i", i=PACK),
            )

        def quantize(codes, scales, values):
            nc.vector.quantize_mx(out=codes.bitcast(FP8X4), scales=scales, in_=values)

        def deal_keys(engine, s0, s1):
            src = k_raw[:].rearrange("p j (s r) -> p s j r", r=PACK)
            cast(engine, k_bf[:].rearrange("p r s j -> p s j r")[:, s0:s1], src[:, s0:s1])

        def quantize_keys(half):
            cols = slice(P // 2 * half, P // 2 * (half + 1))
            for r in range(PACK):
                quantize(k_codes[:, r, cols], k_scales[:, r, cols], k_bf[:, r, cols, :].rearrange("p s j -> p (s j)"))

        def query_cols(i, steps):
            return slice(QB * (i % 2), QB * (i % 2 + steps))

        def cast_queries(engine, i, steps=1):
            cols = query_cols(i, steps)
            interleave(engine, q_bf[i // 2][:, cols, :], q_raw[i // 2][:, :, cols])

        def quantize_queries(i, steps=1):
            cols = query_cols(i, steps)
            values = q_bf[i // 2][:, cols, :].rearrange("p q j -> p (q j)")
            quantize(q_codes[i // 2][:, cols], q_scales[i // 2][:, cols], values)

        def cast_values(engine, g):
            interleave(engine, v_bf[:, g], v_raw[:, g])

        def quantize_values():
            quantize(
                v_codes[:].rearrange("p g e -> p (g e)"),
                v_scales[:].rearrange("p g e -> p (g e)"),
                v_bf[:].rearrange("p g e j -> p (g e j)"),
            )

        def scores(i):
            cols = query_cols(i, 1)
            for r in range(PACK):
                for g in range(2):
                    rows = slice(ROWS * g, ROWS * (g + 1))
                    nc.tensor.matmul_mx(
                        out=score[g][i % 2][:, r, :],
                        lhsT=k_codes[rows, r, :].bitcast(FP8X4),
                        lhsT_scale=k_scales[rows, r, :],
                        rhs=q_codes[i // 2][rows, cols].bitcast(FP8X4),
                        rhs_scale=q_scales[i // 2][rows, cols],
                        start=True,
                        stop=True,
                    )

        def cap(i):
            for g in range(2):
                nc.scalar.activation(
                    out=capped[i][:, g], in_=score[g][i % 2][:].rearrange("p r q -> p q r"), func=ACT.Tanh, scale=0.5
                )

        def weigh(i, g0=0, g1=2):
            nc.vector.scalar_tensor_tensor(
                out=w_bf[i][:, g0:g1].rearrange("p g q r -> p (g q) r"),
                in0=capped[i][:, g0:g1].rearrange("p g q r -> p (g q) r"),
                scalar=0.0,
                in1=t2[:].unsqueeze(1).to_broadcast([P, (g1 - g0) * QB, PACK]),
                op0=ALU.max,
                op1=ALU.mult,
            )

        def quantize_weights(i):
            quantize(
                w_codes[i][:].rearrange("p g q -> p (g q)"),
                w_scales[i][:].rearrange("p g q -> p (g q)"),
                w_bf[i][:].rearrange("p g q r -> p (g q r)"),
            )

        def mix(i):
            for g in range(2):
                nc.tensor.matmul_mx(
                    out=ybank[i // 2][:, i % 2, g, :],
                    lhsT=w_codes[i][:, g, :].bitcast(FP8X4),
                    lhsT_scale=w_scales[i][:, g, :],
                    rhs=v_codes[:, g, :].bitcast(FP8X4),
                    rhs_scale=v_scales[:, g, :],
                    start=True,
                    stop=True,
                )

        def sum_squares(i, heads=(0, 1)):
            for g in heads:
                nc.scalar.activation(
                    out=squares[i][:, g, :],
                    in_=ybank[i // 2][:, i % 2, g, :],
                    func=ACT.Square,
                    accum_out=sums[i // 2][:, i % 2, g : g + 1],
                )

        def norm_factor(c):
            nc.scalar.activation(
                out=factor[c][:], in_=sums[c][:], func=ACT.Abs_reciprocal_sqrt, scale=1.0 / 32.0, bias=1024e-5
            )

        def gate_half_tanh(u):
            nc.scalar.activation(out=gate_tanh[u][:], in_=og_raw[u][:], func=ACT.Tanh, scale=0.5)

        def gate_gain(u, b0=0, b1=BLOCKS):
            nc.vector.scalar_tensor_tensor(
                out=gate[u][:, b0:b1],
                in0=gate_tanh[u][:, b0:b1],
                scalar=1.0,
                in1=gn_sb[:].unsqueeze(1).to_broadcast([P, b1 - b0, E]),
                op0=ALU.add,
                op1=ALU.mult,
            )

        def finish(i):
            pair, rows = PAIRS[i // BLOCKS], slice(QB * (i % BLOCKS), QB * (i % BLOCKS + 1))
            for g in range(2):
                nc.vector.scalar_tensor_tensor(
                    out=result[i][:, g, :],
                    in0=ybank[i // 2][:, i % 2, g, :],
                    scalar=factor[i // 2][:, i % 2, g : g + 1],
                    in1=gate[2 * (i // BLOCKS) + g][:, i % BLOCKS, :],
                    op0=ALU.mult,
                    op1=ALU.mult,
                )
            heads = out[pair[0] : pair[1] + 1 : pair[1] - pair[0], rows, :]
            nc.sync.dma_start(out=heads.rearrange("h q e -> q h e"), in_=result[i][:])

        deal_keys("scalar", KEY_SPLIT, P)
        deal_keys("vector", 0, P // 2)
        deal_keys("vector", P // 2, KEY_SPLIT)
        quantize_keys(0)
        cast_queries("scalar", 1)
        cast_queries("vector", 0)
        quantize_keys(1)
        for i in range(2):
            quantize_queries(i)
            scores(i)
        cast_queries("scalar", 2)
        cast_queries("vector", 3)
        nc.vector.tensor_scalar(out=t2[:], in0=t_raw[:], scalar1=twos[:], scalar2=0.0, op0=ALU.mult, op1=ALU.add)
        quantize_queries(2, steps=2)
        for i in range(2):
            cap(i)
            scores(i + 2)
        cast_values("vector", 1)
        cast_values("vector", 0)
        for i in range(2):
            weigh(i, 0, 1)
            weigh(i, 1, 2)
        cap(2)
        quantize_values()
        cast_queries("vector", 4)
        quantize_weights(0)
        mix(0)
        quantize_queries(4)
        scores(4)
        cast_queries("scalar", 5)
        cap(3)
        weigh(2)
        quantize_queries(5)
        scores(5)
        quantize_weights(1)
        sum_squares(0)
        mix(1)
        cap(4)
        cap(5)
        weigh(3, 0, 1)
        weigh(3, 1, 2)
        cast_queries("vector", 6, steps=2)
        quantize_weights(2)
        quantize_queries(6, steps=2)
        scores(6)
        scores(7)
        mix(2)
        sum_squares(1)
        gate_half_tanh(0)
        gate_half_tanh(1)
        for i in (6, 7):
            cap(i)
            gate_half_tanh(i - 4)
        for i in (4, 5):
            weigh(i)
            quantize_weights(i - 1)
            mix(i - 1)
        gate_gain(0)
        quantize_weights(5)
        mix(5)
        weigh(6)
        gate_gain(1)
        quantize_weights(6)
        mix(6)
        weigh(7)

        norm_factor(0)
        gate_gain(2, 0, 2)
        quantize_weights(7)
        mix(7)
        finish(0)
        finish(1)
        for c in (1, 2):
            sum_squares(2 * c, heads=(0, 1) if c == 1 else (1,))
            sum_squares(2 * c + 1)
            sum_squares(2 * c + 2, heads=(0,))
            norm_factor(c)
        sum_squares(6, heads=(1,))
        sum_squares(7)
        norm_factor(3)
        gate_gain(3, 0, 2)
        finish(2)
        finish(3)
        gate_gain(2, 2, 4)
        finish(4)
        gate_gain(3, 2, 4)
        for i in (5, 6, 7):
            finish(i)
